import numpy as np, ml_dtypes
CORES = [122,123,126,250,251,254,378,379,382,506,507,510]
N = 12
QP = 64
def setup_inputs(rng):
    return {"q": rng.standard_normal((N, 128, QP), dtype=np.float32).astype(ml_dtypes.bfloat16), "k": rng.standard_normal((N, 128, 128), dtype=np.float32).astype(ml_dtypes.bfloat16), "v": rng.standard_normal((N, 128, 128), dtype=np.float32).astype(ml_dtypes.bfloat16), "b": (8 * rng.standard_normal((N, 128, N * QP), dtype=np.float32)).astype(ml_dtypes.bfloat16)}
def setup_inputs_big(rng):
    d = setup_inputs(rng)
    for k in ("q", "k", "v", "b"): d[k] = (d[k].astype(np.float32) * 1024.0).astype(d[k].dtype)
    return d
def setup_inputs_small(rng):
    d = setup_inputs(rng)
    for k in ("q", "k", "v", "b"): d[k] = (d[k].astype(np.float32) * (1 / 1024.0)).astype(d[k].dtype)
    return d
def setup_inputs_apart(rng):
    d = setup_inputs(rng)
    f = (10.0 ** rng.permutation(np.linspace(-1.5, 1.5, N))).astype(np.float32).reshape(N, 1, 1)
    for k in ("q", "k", "v", "b"): d[k] = (d[k].astype(np.float32) * f).astype(d[k].dtype)
    return d
def reference(q, k, v, b):
    Q, K, V, B = q.astype(np.float64), k.astype(np.float64), v.astype(np.float64), b.astype(np.float64)
    y = np.zeros((N, 128, QP))
    for r in range(N):
        for j in range(N):
            y[r] += V[j].T @ np.maximum(K[j].T @ Q[r] + B[r][:, QP * j:QP * j + QP], 0.0)
    return {"y": y.astype(ml_dtypes.bfloat16 if q.dtype != np.float64 else np.float64)}

@@ -1,0 +1,276 @@
+from concourse.bass import DstId, RemoteDMATransfer
+from concourse.mybir import AluOpType
+
+QP = 64
+KP = 128
+HB = 3 * QP
+KV = 2 * KP
+WIN = QP + HB
+M_BS, M_QL, M_K, M_V, M_QR, M_BC, M_END = 0, HB, WIN, WIN + KP, WIN + KV, WIN + KV + QP, 2 * WIN + KV
+NU = 6
+
+SCRATCH = {
+    "main": ("sbuf", [128, M_END], "bfloat16"),
+    "aux": ("sbuf", [128, WIN + HB], "bfloat16"),
+    "kvl": ("sbuf", [128, 3 * KV], "bfloat16"),
+    "pl": ("sbuf", [128, 2 * (KV + WIN)], "bfloat16"),
+    "fl": ("sbuf", [128, 2 * WIN], "bfloat16"),
+    "ol": ("sbuf", [128, 3 * QP], "bfloat16"),
+    "ob": ("sbuf", [128, 4 * QP], "bfloat16"),
+    "s": ("sbuf", [128, NU * HB], "bfloat16"),
+    "zero": ("sbuf", [128, HB], "float32"),
+    "z": ("sbuf", [128, 129], "bfloat16"),
+    "idd": ("dram", [129, 128], "bfloat16"),
+    "ident": ("sbuf", [128, 128], "bfloat16"),
+    "yb": ("sbuf", [128, QP], "bfloat16"),
+    "p0": ("psum", [128, 512], "float32"),
+    "p1": ("psum", [128, 512], "float32"),
+    "p2": ("psum", [128, 512], "float32"),
+    "p3": ("psum", [128, 512], "float32"),
+    "p4": ("psum", [128, 512], "float32"),
+    "pos": ("psum", [128, 512], "float32"),
+    "pof": ("psum", [128, 512], "float32"),
+    "pop": ("psum", [128, 512], "float32"),
+}
+SEMAPHORES = (["ld1", "ld2", "ld3", "ld4", "sz", "szero", "sidd", "sid", "sent", "akv", "afq", "apl", "aoc", "aof",
+               "sof", "sop", "sos", "scf", "scp", "sy", "sst"]
+              + ["t%d" % u for u in range(NU)] + ["r%d" % u for u in range(NU)])
+
+
+def _bits(m):
+    return [e for e in range(m.bit_length()) if (m >> e) & 1]
+
+
+def _layout(T, topo):
+    cores = list(T.cores)
+    hosts = sorted(set(topo.host(c) for c in cores))
+    mem = {h: [c for c in cores if topo.host(c) == h] for h in hosts}
+    L = {}
+    for h in hosts:
+        m = mem[h]
+        near = [x for x in hosts if x != h and topo.may_write(m[0], mem[x][0])]
+        order = sorted(m, key=lambda c: (-len([x for x in m if topo.die(x) == topo.die(c)]), m.index(c)))
+        L[h] = {"sw": [x for x in near if topo.rack(x) == topo.rack(h)][0],
+                "cb": [x for x in near if topo.rack(x) != topo.rack(h)][0],
+                "far": [x for x in hosts if x != h and x not in near][0],
+                "hs": order[0], "hc": order[1], "sp": order[2]}
+    return cores, mem, L
+
+
+def _handler(L, at, of):
+    return L[at]["hs"] if L[at]["sw"] == of else L[at]["hc"]
+
+
+def _target(c, L, topo):
+    me = L[topo.host(c)]
+    return _handler(L, me["sw"] if c == me["hs"] else me["cb"], me["far"])
+
+
+def _guests(x, cores, L, topo):
+    return [r for r in cores if _target(r, L, topo) == x]
+
+
+def _calls(c, cores, mem, L, topo):
+    h = topo.host(c)
+    me, m = L[h], mem[h]
+    peers = [x for x in m if x != c]
+    d_sw, d_cb = _handler(L, me["sw"], h), _handler(L, me["cb"], h)
+    off = _bits(topo.mask(c, d_sw) & topo.mask(c, d_cb))
+    on = [e for e in _bits(topo.mask(c, peers[0]) & topo.mask(c, peers[1])) if e not in off]
+    i = m.index(c)
+
+    def slot(x):
+        return (KV + WIN) * [p for p in m if p != x].index(c)
+
+    out = {}
+    out["kv"] = [(d_sw, "main", M_K, M_QR, "kvl", KV * i, KV * i + KV, "akv", off[0::2]),
+                 (d_cb, "main", M_K, M_QR, "kvl", KV * i, KV * i + KV, "akv", off[1::2])]
+    t = _target(c, L, topo)
+    s = WIN * _guests(t, cores, L, topo).index(c)
+    out["fq"] = [(t, "aux", 0, WIN, "fl", s, s + WIN, "afq", off)]
+    combo = []
+    if c != me["hs"]:
+        combo.append((me["hs"], "main", M_BS, M_QR, "pl", slot(me["hs"]), slot(me["hs"]) + KV + WIN, "apl"))
+    if c != me["hc"]:
+        combo.append((me["hc"], "main", M_K, M_END, "pl", slot(me["hc"]), slot(me["hc"]) + KV + WIN, "apl"))
+    out["combo"] = [tr + (on[n::len(combo)],) for n, tr in enumerate(combo)]
+    if c != me["sp"]:
+        out["kvp"] = [(me["sp"], "main", M_K, M_QR, "pl", slot(me["sp"]), slot(me["sp"]) + KV, "apl", on)]
+        gs = _guests(c, cores, L, topo)
+        out["of"] = [(r, "ob", QP * n, QP * n + QP, "ol", 2 * QP, 3 * QP, "aof", off[n::len(gs)])
+                     for n, r in enumerate(gs)]
+        w = 0 if c == me["hs"] else QP
+        out["op"] = [(p, "ob", 2 * QP + QP * n, 3 * QP + QP * n, "ol", w, w + QP, "aoc", on[n::2])
+                     for n, p in enumerate(peers)]
+    return out
+
+
+def rank_program(g, core, T, topo):
+    if T.rank_of(core) is None:
+        return
+    cores, mem, L = _layout(T, topo)
+    h = topo.host(core)
+    me, m = L[h], mem[h]
+    peers = [x for x in m if x != core]
+    role = "hs" if core == me["hs"] else ("hc" if core == me["hc"] else "sp")
+    sem = T.sem
+    mine = _calls(core, cores, mem, L, topo)
+    everyone = [tr for c in cores for trs in _calls(c, cores, mem, L, topo).values() for tr in trs]
+
+    def expect(name):
+        return sum(len(tr[8]) for tr in everyone if tr[0] == core and tr[7] == name)
+
+    def emit(name):
+        trs = []
+        for (d, sb, s0, s1, db, d0, d1, sn, eng) in mine[name]:
+            rid, pid = topo.addr(d, core)
+            trs.append(RemoteDMATransfer(dst_ids=[DstId(rid=rid, pnc=pid)], dma_engine_mask=sum(1 << e for e in eng),
+                                         remote_sem=sem[sn], src=T[sb][:, s0:s1], dst=T[db][:, d0:d1]))
+        g.remote_dma_fused(trs, local_sem=sem.sent)
+
+    def bsrc(host):
+        c0 = QP * T.rank_of(mem[host][0])
+        return T.b[:, c0:c0 + HB]
+
+    te, ve = g.tensor, g.vector
+
+    ve.memset(T.z[:, 0:1], 1.0).then_inc(sem.sz, 1)
+    ve.memset(T.z[:, 1:129], 0.0).then_inc(sem.sz, 1)
+    ve.memset(T.zero[:], 0.0).then_inc(sem.szero, 1)
+
+    g.sync.dma_start(T.main[:, M_K:M_V], T.k[:]).then_inc(sem.ld1, 16)
+    g.scalar.dma_start(T.main[:, M_V:M_QR], T.v[:]).then_inc(sem.ld1, 16)
+    g.sync.dma_start(T.aux[:, 0:QP], T.q[:]).then_inc(sem.ld2, 16)
+    g.scalar.dma_start(T.aux[:, QP:WIN], bsrc(me["far"])).then_inc(sem.ld2, 16)
+    n3 = 0
+    if role != "hs":
+        g.sync.dma_start(T.main[:, M_QL:M_K], T.q[:]).then_inc(sem.ld3, 16)
+        g.scalar.dma_start(T.main[:, M_BS:M_QL], bsrc(me["sw"])).then_inc(sem.ld3, 16)
+        n3 += 32
+    if role != "hc":
+        g.sync.dma_start(T.main[:, M_QR:M_BC], T.q[:]).then_inc(sem.ld3, 16)
+        g.scalar.dma_start(T.main[:, M_BC:M_END], bsrc(me["cb"])).then_inc(sem.ld3, 16)
+        n3 += 32
+    g.sync.wait_ge(sem.sz, 2)
+    g.sync.dma_start(T.idd[:], T.z[:]).then_inc(sem.sidd, 16)
+    n4 = 16
+    g.scalar.dma_start(T.aux[:, WIN:WIN + HB], bsrc(h)).then_inc(sem.ld4, 16)
+    if role == "hs":
+        g.scalar.dma_start(T.main[:, M_BS:M_QL], bsrc(me["sw"])).then_inc(sem.ld4, 16)
+        n4 += 16
+    if role == "hc":
+        g.scalar.dma_start(T.main[:, M_BC:M_END], bsrc(me["cb"])).then_inc(sem.ld4, 16)
+        n4 += 16
+    g.sync.wait_ge(sem.sidd, 16)
+    g.sync.dma_start(T.ident[:], T.idd[0:128, :]).then_inc(sem.sid, 16)
+
+    g.wait_ge(sem.ld1, 32)
+    emit("kv")
+    g.wait_ge(sem.ld2, 32)
+    emit("fq")
+    g.wait_ge(sem.ld3, n3)
+    emit("combo")
+    if role != "sp":
+        emit("kvp")
+
+    def cols(buf, c0, n):
+        return T[buf][:, c0:c0 + n]
+
+    po = KV + WIN
+    pk = WIN if role == "hs" else 0
+    pq, pb = (HB, 0) if role == "hs" else (KV, KV + QP)
+    kv_own = []
+    for x in m:
+        if x == core:
+            kv_own.append((cols("main", M_K, KP), cols("main", M_V, KP)))
+        else:
+            o = po * peers.index(x) + pk
+            kv_own.append((cols("pl", o, KP), cols("pl", o + KP, KP)))
+    kv_j = [(cols("kvl", KV * j, KP), cols("kvl", KV * j + KP, KP)) for j in range(3)]
+    q_me = cols("aux", 0, QP)
+
+    def bias(u, bank, b):
+        te.matmul(T[bank][:, 0:HB], T.ident[:], b, True, False).then_inc(sem["t%d" % u], 1)
+
+    def scores(u, bank, q, kv):
+        for j in range(3):
+            te.matmul(T[bank][:, QP * j:QP * j + QP], kv[j][0], q, False, j == 2).then_inc(sem["t%d" % u], 1)
+
+    def clamp(u, bank):
+        ve.wait_ge(sem["t%d" % u], 4)
+        ve.tensor_tensor(cols("s", HB * u, HB), T[bank][:, 0:HB], T.zero[:], AluOpType.max).then_inc(sem["r%d" % u], 1)
+
+    def values(u, out, kv, done, first, last):
+        te.wait_ge(sem["r%d" % u], 1)
+        for j in range(3):
+            te.matmul(out, kv[j][1], cols("s", HB * u + QP * j, QP), first and j == 0, last and j == 2).then_inc(done, 1)
+
+    y_acc = T.pos[:, 0:QP]
+    n_in = (1 if role != "sp" else 2) + 1
+    n_y = 0
+    te.wait_ge(sem.sid, 16)
+    ve.wait_ge(sem.szero, 1)
+    if role != "sp":
+        gs = _guests(core, cores, L, topo)
+        b_me = cols("main", M_BS, HB) if role == "hs" else cols("main", M_BC, HB)
+        te.wait_ge(sem.ld2, 32)
+        te.wait_ge(sem.ld4, n4)
+        bias(4, "p4", b_me)
+        te.wait_ge(sem.afq, expect("afq"))
+        for n in range(len(gs)):
+            bias(n, "p%d" % n, cols("fl", WIN * n + QP, HB))
+        te.wait_ge(sem.akv, expect("akv"))
+        for n in range(len(gs)):
+            scores(n, "p%d" % n, cols("fl", WIN * n, QP), kv_j)
+            clamp(n, "p%d" % n)
+        for n in range(len(gs)):
+            values(n, T.pof[:, QP * n:QP * n + QP], kv_j, sem.sof, True, True)
+        ve.wait_ge(sem.sof, 3 * len(gs))
+        ve.tensor_copy(T.ob[:, 0:QP * len(gs)], T.pof[:, 0:QP * len(gs)]).then_inc(sem.scf, 1)
+        g.wait_ge(sem.scf, 1)
+        emit("of")
+        te.wait_ge(sem.apl, expect("apl"))
+        for n in range(2):
+            bias(2 + n, "p%d" % (2 + n), cols("pl", po * n + pb, HB))
+            scores(2 + n, "p%d" % (2 + n), cols("pl", po * n + pq, QP), kv_j)
+            clamp(2 + n, "p%d" % (2 + n))
+        scores(4, "p4", q_me, kv_j)
+        for n in range(2):
+            values(2 + n, T.pop[:, QP * n:QP * n + QP], kv_j, sem.sop, True, True)
+        ve.wait_ge(sem.sop, 6)
+        ve.tensor_copy(T.ob[:, 2 * QP:4 * QP], T.pop[:, 0:2 * QP]).then_inc(sem.scp, 1)
+        g.wait_ge(sem.scp, 1)
+        emit("op")
+        clamp(4, "p4")
+        te.wait_ge(sem.ld1, 32)
+        bias(5, "p0", cols("aux", WIN, HB))
+        scores(5, "p0", q_me, kv_own)
+        clamp(5, "p0")
+        values(4, y_acc, kv_j, sem.sos, True, False)
+        values(5, y_acc, kv_own, sem.sos, False, False)
+        n_y += 6
+    else:
+        te.wait_ge(sem.ld2, 32)
+        te.wait_ge(sem.ld4, n4)
+        bias(5, "p0", cols("aux", WIN, HB))
+        te.wait_ge(sem.ld1, 32)
+        te.wait_ge(sem.apl, expect("apl"))
+        scores(5, "p0", q_me, kv_own)
+        clamp(5, "p0")
+        values(5, y_acc, kv_own, sem.sos, True, False)
+        n_y += 3
+
+    te.wait_ge(sem.aoc, expect("aoc"))
+    for w, hd in enumerate(("hs", "hc")):
+        if role != hd:
+            te.matmul(y_acc, T.ident[:], cols("ol", QP * w, QP), False, False).then_inc(sem.sos, 1)
+            n_y += 1
+    te.wait_ge(sem.aof, expect("aof"))
+    te.matmul(y_acc, T.ident[:], cols("ol", 2 * QP, QP), False, True).then_inc(sem.sos, 1)
+    n_y += 1
+    ve.wait_ge(sem.sos, n_y)
+    ve.tensor_copy(T.yb[:], y_acc).then_inc(sem.sy, 1)
+    g.sync.wait_ge(sem.sy, 1)
+    g.sync.dma_start(T.y[:], T.yb[:]).then_inc(sem.sst, 16)
+    g.sync.wait_ge(sem.sst, 16)
+    g.wait_ge(sem.sent, sum(len(tr[8]) for trs in mine.values() for tr in trs))

@@ -6,22 +6,23 @@ KP = 128
 HB = 3 * QP
 KV = 2 * KP
 WIN = QP + HB
-M_BS, M_QL, M_K, M_V, M_QR, M_BC, M_END = 0, HB, WIN, WIN + KP, WIN + KV, WIN + KV + QP, 2 * WIN + KV
 NU = 6
 
 SCRATCH = {
-    "main": ("sbuf", [128, M_END], "bfloat16"),
-    "aux": ("sbuf", [128, WIN + HB], "bfloat16"),
+    "kv": ("sbuf", [128, KV], "bfloat16"),
+    "aux": ("sbuf", [128, HB + WIN], "bfloat16"),
+    "aux2": ("sbuf", [128, WIN], "bfloat16"),
+    "rest": ("sbuf", [128, 2 * HB], "bfloat16"),
     "kvl": ("sbuf", [128, 3 * KV], "bfloat16"),
-    "pl": ("sbuf", [128, 2 * (KV + WIN)], "bfloat16"),
+    "pk": ("sbuf", [128, 2 * KV], "bfloat16"),
+    "pw": ("sbuf", [128, 2 * WIN], "bfloat16"),
     "fl": ("sbuf", [128, 2 * WIN], "bfloat16"),
     "ol": ("sbuf", [128, 3 * QP], "bfloat16"),
     "ob": ("sbuf", [128, 4 * QP], "bfloat16"),
     "s": ("sbuf", [128, NU * HB], "bfloat16"),
     "zero": ("sbuf", [128, HB], "float32"),
-    "z": ("sbuf", [128, 129], "bfloat16"),
-    "idd": ("dram", [129, 128], "bfloat16"),
-    "ident": ("sbuf", [128, 128], "bfloat16"),
+    "ones": ("sbuf", [128, KP], "bfloat16"),
+    "ident": ("sbuf", [128, KP], "bfloat16"),
     "yb": ("sbuf", [128, QP], "bfloat16"),
     "p0": ("psum", [128, 512], "float32"),
     "p1": ("psum", [128, 512], "float32"),
@@ -32,7 +33,7 @@ SCRATCH = {
     "pof": ("psum", [128, 512], "float32"),
     "pop": ("psum", [128, 512], "float32"),
 }
-SEMAPHORES = (["ld1", "ld2", "ld3", "ld4", "sz", "szero", "sidd", "sid", "sent", "akv", "afq", "apl", "aoc", "aof",
+SEMAPHORES = (["ld1", "ld2", "ld3", "ld4", "sz", "szero", "sid", "sent", "akv", "afq", "apk", "apw", "aoc0", "aoc1", "aof",
                "sof", "sop", "sos", "scf", "scp", "sy", "sst"]
               + ["t%d" % u for u in range(NU)] + ["r%d" % u for u in range(NU)])
 
@@ -63,7 +64,7 @@ def _handler(L, at, of):
 
 def _target(c, L, topo):
     me = L[topo.host(c)]
-    return _handler(L, me["sw"] if c == me["hs"] else me["cb"], me["far"])
+    return _handler(L, me["cb"] if c == me["sp"] else me["sw"], me["far"])
 
 
 def _guests(x, cores, L, topo):
@@ -75,32 +76,35 @@ def _calls(c, cores, mem, L, topo):
     me, m = L[h], mem[h]
     peers = [x for x in m if x != c]
     d_sw, d_cb = _handler(L, me["sw"], h), _handler(L, me["cb"], h)
-    off = _bits(topo.mask(c, d_sw) & topo.mask(c, d_cb))
-    on = [e for e in _bits(topo.mask(c, peers[0]) & topo.mask(c, peers[1])) if e not in off]
+    chip = _bits(topo.mask(c, peers[0]) & topo.mask(c, peers[1]))
+    off = [e for e in _bits(topo.mask(c, d_sw) & topo.mask(c, d_cb)) if e in chip]
+    on = [e for e in chip if e not in off]
+    half = len(off) // 2
     i = m.index(c)
 
     def slot(x):
-        return (KV + WIN) * [p for p in m if p != x].index(c)
+        return [p for p in m if p != x].index(c)
 
     out = {}
-    out["kv"] = [(d_sw, "main", M_K, M_QR, "kvl", KV * i, KV * i + KV, "akv", off[0::2]),
-                 (d_cb, "main", M_K, M_QR, "kvl", KV * i, KV * i + KV, "akv", off[1::2])]
+    out["kvs"] = [(d_sw, "kv", 0, KV, "kvl", KV * i, KV * i + KV, "akv", off[0:half:2])]
+    out["kvc"] = [(d_cb, "kv", 0, KV, "kvl", KV * i, KV * i + KV, "akv", off[1:half:2])]
     t = _target(c, L, topo)
     s = WIN * _guests(t, cores, L, topo).index(c)
-    out["fq"] = [(t, "aux", 0, WIN, "fl", s, s + WIN, "afq", off)]
-    combo = []
-    if c != me["hs"]:
-        combo.append((me["hs"], "main", M_BS, M_QR, "pl", slot(me["hs"]), slot(me["hs"]) + KV + WIN, "apl"))
+    out["fq"] = [(t, "aux", 0, WIN, "fl", s, s + WIN, "afq", off[half:])]
+    win = []
     if c != me["hc"]:
-        combo.append((me["hc"], "main", M_K, M_END, "pl", slot(me["hc"]), slot(me["hc"]) + KV + WIN, "apl"))
-    out["combo"] = [tr + (on[n::len(combo)],) for n, tr in enumerate(combo)]
+        win.append((me["hc"], "aux", HB, HB + WIN))
+    if c != me["hs"]:
+        win.append((me["hs"], "aux", HB, HB + WIN) if c == me["hc"] else (me["hs"], "aux2", 0, WIN))
+    out["win"] = [(x, sb, s0, s1, "pw", WIN * slot(x), WIN * slot(x) + WIN, "apw", off[n::len(win)])
+                  for n, (x, sb, s0, s1) in enumerate(win)]
+    out["kvp"] = [(p, "kv", 0, KV, "pk", KV * slot(p), KV * slot(p) + KV, "apk", on[n::2]) for n, p in enumerate(peers)]
     if c != me["sp"]:
-        out["kvp"] = [(me["sp"], "main", M_K, M_QR, "pl", slot(me["sp"]), slot(me["sp"]) + KV, "apl", on)]
         gs = _guests(c, cores, L, topo)
         out["of"] = [(r, "ob", QP * n, QP * n + QP, "ol", 2 * QP, 3 * QP, "aof", off[n::len(gs)])
                      for n, r in enumerate(gs)]
-        w = 0 if c == me["hs"] else QP
-        out["op"] = [(p, "ob", 2 * QP + QP * n, 3 * QP + QP * n, "ol", w, w + QP, "aoc", on[n::2])
+        w = 0 if c == me["hs"] else 1
+        out["op"] = [(p, "ob", 2 * QP + QP * n, 3 * QP + QP * n, "ol", QP * w, QP * w + QP, "aoc%d" % w, on[n::2])
                      for n, p in enumerate(peers)]
     return out
 
@@ -128,66 +132,66 @@ def rank_program(g, core, T, topo):
                                          remote_sem=sem[sn], src=T[sb][:, s0:s1], dst=T[db][:, d0:d1]))
         g.remote_dma_fused(trs, local_sem=sem.sent)
 
-    def bsrc(host):
-        c0 = QP * T.rank_of(mem[host][0])
-        return T.b[:, c0:c0 + HB]
+    def bcol(host):
+        return QP * T.rank_of(mem[host][0])
+
+    def bsrc(host, n=1):
+        return T.b[:, bcol(host):bcol(host) + n * HB]
 
     te, ve = g.tensor, g.vector
 
-    ve.memset(T.z[:, 0:1], 1.0).then_inc(sem.sz, 1)
-    ve.memset(T.z[:, 1:129], 0.0).then_inc(sem.sz, 1)
+    ve.memset(T.ones[:], 1.0).then_inc(sem.sz, 1)
     ve.memset(T.zero[:], 0.0).then_inc(sem.szero, 1)
+    g.wait_ge(sem.sz, 1)
+    g.affine_select(T.ident[:], T.ones[:], [[-1, KP]], AluOpType.is_equal, 0.0, 0, 1).then_inc(sem.sid, 1)
 
-    g.sync.dma_start(T.main[:, M_K:M_V], T.k[:]).then_inc(sem.ld1, 16)
-    g.scalar.dma_start(T.main[:, M_V:M_QR], T.v[:]).then_inc(sem.ld1, 16)
-    g.sync.dma_start(T.aux[:, 0:QP], T.q[:]).then_inc(sem.ld2, 16)
-    g.scalar.dma_start(T.aux[:, QP:WIN], bsrc(me["far"])).then_inc(sem.ld2, 16)
-    n3 = 0
-    if role != "hs":
-        g.sync.dma_start(T.main[:, M_QL:M_K], T.q[:]).then_inc(sem.ld3, 16)
-        g.scalar.dma_start(T.main[:, M_BS:M_QL], bsrc(me["sw"])).then_inc(sem.ld3, 16)
+    g.sync.dma_start(T.kv[:, 0:KP], T.k[:]).then_inc(sem.ld1, 16)
+    g.scalar.dma_start(T.kv[:, KP:KV], T.v[:]).then_inc(sem.ld1, 16)
+    g.sync.dma_start(T.aux[:, HB:WIN], T.q[:]).then_inc(sem.ld2, 16)
+    g.scalar.dma_start(T.aux[:, 0:HB], bsrc(me["far"])).then_inc(sem.ld2, 16)
+    g.sync.dma_start(T.aux[:, WIN:WIN + HB], bsrc(me["sw"] if role == "hc" else me["cb"])).then_inc(sem.ld3, 16)
+    n3, n4 = 16, 0
+    where = {}
+    if role == "sp":
+        g.scalar.dma_start(T.aux2[:, 0:QP], T.q[:]).then_inc(sem.ld3, 16)
+        g.sync.dma_start(T.aux2[:, QP:WIN], bsrc(me["sw"])).then_inc(sem.ld3, 16)
         n3 += 32
-    if role != "hc":
-        g.sync.dma_start(T.main[:, M_QR:M_BC], T.q[:]).then_inc(sem.ld3, 16)
-        g.scalar.dma_start(T.main[:, M_BC:M_END], bsrc(me["cb"])).then_inc(sem.ld3, 16)
-        n3 += 32
-    g.sync.wait_ge(sem.sz, 2)
-    g.sync.dma_start(T.idd[:], T.z[:]).then_inc(sem.sidd, 16)
-    n4 = 16
-    g.scalar.dma_start(T.aux[:, WIN:WIN + HB], bsrc(h)).then_inc(sem.ld4, 16)
-    if role == "hs":
-        g.scalar.dma_start(T.main[:, M_BS:M_QL], bsrc(me["sw"])).then_inc(sem.ld4, 16)
+        g.scalar.dma_start(T.rest[:, 0:HB], bsrc(h)).then_inc(sem.ld4, 16)
         n4 += 16
-    if role == "hc":
-        g.scalar.dma_start(T.main[:, M_BC:M_END], bsrc(me["cb"])).then_inc(sem.ld4, 16)
-        n4 += 16
-    g.sync.wait_ge(sem.sidd, 16)
-    g.sync.dma_start(T.ident[:], T.idd[0:128, :]).then_inc(sem.sid, 16)
+        where[h] = 0
+    else:
+        stay = sorted([h, me["sw"] if role == "hs" else me["cb"]], key=bcol)
+        where[stay[0]], where[stay[1]] = 0, HB
+        if bcol(stay[1]) - bcol(stay[0]) == HB:
+            g.scalar.dma_start(T.rest[:], bsrc(stay[0], 2)).then_inc(sem.ld4, 16)
+            n4 += 16
+        else:
+            g.scalar.dma_start(T.rest[:, 0:HB], bsrc(stay[0])).then_inc(sem.ld4, 16)
+            g.sync.dma_start(T.rest[:, HB:2 * HB], bsrc(stay[1])).then_inc(sem.ld4, 16)
+            n4 += 32
 
     g.wait_ge(sem.ld1, 32)
-    emit("kv")
+    emit("kvc")
+    emit("kvs")
     g.wait_ge(sem.ld2, 32)
     emit("fq")
     g.wait_ge(sem.ld3, n3)
-    emit("combo")
-    if role != "sp":
-        emit("kvp")
+    emit("win")
+    emit("kvp")
 
     def cols(buf, c0, n):
         return T[buf][:, c0:c0 + n]
 
-    po = KV + WIN
-    pk = WIN if role == "hs" else 0
-    pq, pb = (HB, 0) if role == "hs" else (KV, KV + QP)
     kv_own = []
     for x in m:
         if x == core:
-            kv_own.append((cols("main", M_K, KP), cols("main", M_V, KP)))
+            kv_own.append((cols("kv", 0, KP), cols("kv", KP, KP)))
         else:
-            o = po * peers.index(x) + pk
-            kv_own.append((cols("pl", o, KP), cols("pl", o + KP, KP)))
+            o = KV * peers.index(x)
+            kv_own.append((cols("pk", o, KP), cols("pk", o + KP, KP)))
     kv_j = [(cols("kvl", KV * j, KP), cols("kvl", KV * j + KP, KP)) for j in range(3)]
-    q_me = cols("aux", 0, QP)
+    q_me = cols("aux", HB, QP)
+    b_own = cols("rest", where[h], HB)
 
     def bias(u, bank, b):
         te.matmul(T[bank][:, 0:HB], T.ident[:], b, True, False).then_inc(sem["t%d" % u], 1)
@@ -206,70 +210,74 @@ def rank_program(g, core, T, topo):
             te.matmul(out, kv[j][1], cols("s", HB * u + QP * j, QP), first and j == 0, last and j == 2).then_inc(done, 1)
 
     y_acc = T.pos[:, 0:QP]
-    n_in = (1 if role != "sp" else 2) + 1
     n_y = 0
-    te.wait_ge(sem.sid, 16)
+    te.wait_ge(sem.sid, 1)
     ve.wait_ge(sem.szero, 1)
+    te.wait_ge(sem.ld2, 32)
+    te.wait_ge(sem.ld4, n4)
     if role != "sp":
         gs = _guests(core, cores, L, topo)
-        b_me = cols("main", M_BS, HB) if role == "hs" else cols("main", M_BC, HB)
-        te.wait_ge(sem.ld2, 32)
-        te.wait_ge(sem.ld4, n4)
+        b_me = cols("rest", where[me["sw"] if role == "hs" else me["cb"]], HB)
         bias(4, "p4", b_me)
         te.wait_ge(sem.afq, expect("afq"))
         for n in range(len(gs)):
-            bias(n, "p%d" % n, cols("fl", WIN * n + QP, HB))
+            bias(n, "p%d" % n, cols("fl", WIN * n, HB))
         te.wait_ge(sem.akv, expect("akv"))
         for n in range(len(gs)):
-            scores(n, "p%d" % n, cols("fl", WIN * n, QP), kv_j)
+            scores(n, "p%d" % n, cols("fl", WIN * n + HB, QP), kv_j)
             clamp(n, "p%d" % n)
+        if len(gs) == 1:
+            scores(4, "p4", q_me, kv_j)
         for n in range(len(gs)):
             values(n, T.pof[:, QP * n:QP * n + QP], kv_j, sem.sof, True, True)
         ve.wait_ge(sem.sof, 3 * len(gs))
         ve.tensor_copy(T.ob[:, 0:QP * len(gs)], T.pof[:, 0:QP * len(gs)]).then_inc(sem.scf, 1)
         g.wait_ge(sem.scf, 1)
         emit("of")
-        te.wait_ge(sem.apl, expect("apl"))
+        te.wait_ge(sem.apw, expect("apw"))
         for n in range(2):
-            bias(2 + n, "p%d" % (2 + n), cols("pl", po * n + pb, HB))
-            scores(2 + n, "p%d" % (2 + n), cols("pl", po * n + pq, QP), kv_j)
+            bias(2 + n, "p%d" % (2 + n), cols("pw", WIN * n + QP, HB))
+            scores(2 + n, "p%d" % (2 + n), cols("pw", WIN * n, QP), kv_j)
             clamp(2 + n, "p%d" % (2 + n))
-        scores(4, "p4", q_me, kv_j)
         for n in range(2):
             values(2 + n, T.pop[:, QP * n:QP * n + QP], kv_j, sem.sop, True, True)
         ve.wait_ge(sem.sop, 6)
         ve.tensor_copy(T.ob[:, 2 * QP:4 * QP], T.pop[:, 0:2 * QP]).then_inc(sem.scp, 1)
         g.wait_ge(sem.scp, 1)
         emit("op")
+        if len(gs) != 1:
+            scores(4, "p4", q_me, kv_j)
         clamp(4, "p4")
         te.wait_ge(sem.ld1, 32)
-        bias(5, "p0", cols("aux", WIN, HB))
+        te.wait_ge(sem.apk, expect("apk"))
+        bias(5, "p0", b_own)
         scores(5, "p0", q_me, kv_own)
         clamp(5, "p0")
         values(4, y_acc, kv_j, sem.sos, True, False)
         values(5, y_acc, kv_own, sem.sos, False, False)
         n_y += 6
     else:
-        te.wait_ge(sem.ld2, 32)
-        te.wait_ge(sem.ld4, n4)
-        bias(5, "p0", cols("aux", WIN, HB))
+        bias(5, "p0", b_own)
         te.wait_ge(sem.ld1, 32)
-        te.wait_ge(sem.apl, expect("apl"))
+        te.wait_ge(sem.apk, expect("apk"))
         scores(5, "p0", q_me, kv_own)
         clamp(5, "p0")
         values(5, y_acc, kv_own, sem.sos, True, False)
         n_y += 3
 
-    te.wait_ge(sem.aoc, expect("aoc"))
-    for w, hd in enumerate(("hs", "hc")):
-        if role != hd:
-            te.matmul(y_acc, T.ident[:], cols("ol", QP * w, QP), False, False).then_inc(sem.sos, 1)
-            n_y += 1
+    late = 0 if len(_guests(me["hs"], cores, L, topo)) >= len(_guests(me["hc"], cores, L, topo)) else 1
+    idx = {"hs": 0, "hc": 1, "sp": 2}[role]
+    last = late if idx != late else 1 - late
+    if role == "sp":
+        te.wait_ge(sem["aoc%d" % (1 - late)], expect("aoc%d" % (1 - late)))
+        te.matmul(y_acc, T.ident[:], cols("ol", QP * (1 - late), QP), False, False).then_inc(sem.sos, 1)
+        n_y += 1
     te.wait_ge(sem.aof, expect("aof"))
     te.matmul(y_acc, T.ident[:], cols("ol", 2 * QP, QP), False, True).then_inc(sem.sos, 1)
     n_y += 1
     ve.wait_ge(sem.sos, n_y)
-    ve.tensor_copy(T.yb[:], y_acc).then_inc(sem.sy, 1)
+    ve.wait_ge(sem["aoc%d" % last], expect("aoc%d" % last))
+    ve.tensor_tensor(T.yb[:], y_acc, cols("ol", QP * last, QP), AluOpType.add).then_inc(sem.sy, 1)
     g.sync.wait_ge(sem.sy, 1)
     g.sync.dma_start(T.y[:], T.yb[:]).then_inc(sem.sst, 16)
     g.sync.wait_ge(sem.sst, 16)

@@ -6,7 +6,9 @@ KP = 128
 HB = 3 * QP
 KV = 2 * KP
 WIN = QP + HB
-NU = 6
+GM = 3
+NU = GM + 4
+U_ME, U_OWN = GM + 2, GM + 3
 
 SCRATCH = {
     "kv": ("sbuf", [128, KV], "bfloat16"),
@@ -16,9 +18,9 @@ SCRATCH = {
     "kvl": ("sbuf", [128, 3 * KV], "bfloat16"),
     "pk": ("sbuf", [128, 2 * KV], "bfloat16"),
     "pw": ("sbuf", [128, 2 * WIN], "bfloat16"),
-    "fl": ("sbuf", [128, 2 * WIN], "bfloat16"),
+    "fl": ("sbuf", [128, GM * WIN], "bfloat16"),
     "ol": ("sbuf", [128, 3 * QP], "bfloat16"),
-    "ob": ("sbuf", [128, 4 * QP], "bfloat16"),
+    "ob": ("sbuf", [128, (GM + 2) * QP], "bfloat16"),
     "s": ("sbuf", [128, NU * HB], "bfloat16"),
     "zero": ("sbuf", [128, HB], "float32"),
     "ones": ("sbuf", [128, KP], "bfloat16"),
@@ -33,13 +35,25 @@ SCRATCH = {
     "pof": ("psum", [128, 512], "float32"),
     "pop": ("psum", [128, 512], "float32"),
 }
-SEMAPHORES = (["ld1", "ld2", "ld3", "ld4", "sz", "szero", "sid", "sent", "akv", "afq", "apk", "apw", "aoc0", "aoc1", "aof",
-               "sof", "sop", "sos", "scf", "scp", "sy", "sst"]
+SEMAPHORES = (["ldk", "ldv", "ld2", "ld3", "ld4", "sz", "szero", "sid", "sent", "akv", "ak", "av", "arl", "afq", "apk",
+               "apw", "aoc0", "aoc1", "aof", "sof", "sop", "sos", "scf", "scp", "sy", "sst"]
               + ["t%d" % u for u in range(NU)] + ["r%d" % u for u in range(NU)])
 
 
 def _bits(m):
     return [e for e in range(m.bit_length()) if (m >> e) & 1]
+
+
+def _chip_cores(c, topo):
+    def here(x):
+        return x >= 0 and (topo.host(x), topo.chip(x)) == (topo.host(c), topo.chip(c))
+    lo, hi = c, c
+    while here(lo - 1):
+        lo -= 1
+    while here(hi + 1):
+        hi += 1
+    mate = [x for x in (lo - 1, hi + 1) if x >= 0 and topo.mates(c, x)][0]
+    return list(range(lo, hi + 1)), mate
 
 
 def _layout(T, topo):
@@ -51,10 +65,23 @@ def _layout(T, topo):
         m = mem[h]
         near = [x for x in hosts if x != h and topo.may_write(m[0], mem[x][0])]
         order = sorted(m, key=lambda c: (-len([x for x in m if topo.die(x) == topo.die(c)]), m.index(c)))
+        chip, mate = _chip_cores(m[0], topo)
+
+        def pair(x):
+            return (topo.die(x), topo.may_write(x, mate))
+
+        taken = [pair(x) for x in m]
+        free = []
+        for x in chip:
+            if pair(x) not in taken:
+                taken.append(pair(x))
+                free.append(x)
+        free.sort(key=lambda x: topo.die(x) != topo.die(order[0]))
         L[h] = {"sw": [x for x in near if topo.rack(x) == topo.rack(h)][0],
                 "cb": [x for x in near if topo.rack(x) != topo.rack(h)][0],
                 "far": [x for x in hosts if x != h and x not in near][0],
-                "hs": order[0], "hc": order[1], "sp": order[2]}
+                "hs": order[0], "hc": order[1], "sp": order[2],
+                "relay": {order[0]: free[0], order[1]: free[1]}}
     return cores, mem, L
 
 
@@ -64,7 +91,7 @@ def _handler(L, at, of):
 
 def _target(c, L, topo):
     me = L[topo.host(c)]
-    return _handler(L, me["cb"] if c == me["sp"] else me["sw"], me["far"])
+    return _handler(L, me["sw"], me["far"])
 
 
 def _guests(x, cores, L, topo):
@@ -87,7 +114,11 @@ def _calls(c, cores, mem, L, topo):
 
     out = {}
     out["kvs"] = [(d_sw, "kv", 0, KV, "kvl", KV * i, KV * i + KV, "akv", off[0:half:2])]
-    out["kvc"] = [(d_cb, "kv", 0, KV, "kvl", KV * i, KV * i + KV, "akv", off[1:half:2])]
+    if c == me["sp"]:
+        out["kc"] = [(d_cb, "kv", 0, KV, "kvl", KV * i, KV * i + KV, "ak", off[1:half:2])]
+    else:
+        out["kc"] = [(d_cb, "kv", 0, KP, "kvl", KV * i, KV * i + KP, "ak", off[1:half:2])]
+        out["vr"] = [(me["relay"][c], "kv", KP, KV, "kv", KP, KV, "arl", on[0::2])]
     t = _target(c, L, topo)
     s = WIN * _guests(t, cores, L, topo).index(c)
     out["fq"] = [(t, "aux", 0, WIN, "fl", s, s + WIN, "afq", off[half:])]
@@ -101,25 +132,33 @@ def _calls(c, cores, mem, L, topo):
     out["kvp"] = [(p, "kv", 0, KV, "pk", KV * slot(p), KV * slot(p) + KV, "apk", on[n::2]) for n, p in enumerate(peers)]
     if c != me["sp"]:
         gs = _guests(c, cores, L, topo)
-        out["of"] = [(r, "ob", QP * n, QP * n + QP, "ol", 2 * QP, 3 * QP, "aof", off[n::len(gs)])
-                     for n, r in enumerate(gs)]
+        if gs:
+            out["of"] = [(r, "ob", QP * n, QP * n + QP, "ol", 2 * QP, 3 * QP, "aof", off[2 * n:2 * n + 2])
+                         for n, r in enumerate(gs)]
         w = 0 if c == me["hs"] else 1
-        out["op"] = [(p, "ob", 2 * QP + QP * n, 3 * QP + QP * n, "ol", QP * w, QP * w + QP, "aoc%d" % w, on[n::2])
+        out["op"] = [(p, "ob", QP * (GM + n), QP * (GM + n + 1), "ol", QP * w, QP * w + QP, "aoc%d" % w, on[n::2])
                      for n, p in enumerate(peers)]
     return out
 
 
+def _plan(cores, mem, L, topo):
+    plan = {c: _calls(c, cores, mem, L, topo) for c in cores}
+    for h in L:
+        d_cb = _handler(L, L[h]["cb"], h)
+        for r, x in L[h]["relay"].items():
+            o = KV * mem[h].index(r) + KP
+            plan[x] = {"fw": [(d_cb, "kv", KP, KV, "kvl", o, o + KP, "av", _bits(topo.mask(x, d_cb))[0:4])]}
+    return plan
+
+
 def rank_program(g, core, T, topo):
-    if T.rank_of(core) is None:
-        return
     cores, mem, L = _layout(T, topo)
-    h = topo.host(core)
-    me, m = L[h], mem[h]
-    peers = [x for x in m if x != core]
-    role = "hs" if core == me["hs"] else ("hc" if core == me["hc"] else "sp")
+    plan = _plan(cores, mem, L, topo)
+    if core not in plan:
+        return
     sem = T.sem
-    mine = _calls(core, cores, mem, L, topo)
-    everyone = [tr for c in cores for trs in _calls(c, cores, mem, L, topo).values() for tr in trs]
+    mine = plan[core]
+    everyone = [tr for calls in plan.values() for trs in calls.values() for tr in trs]
 
     def expect(name):
         return sum(len(tr[8]) for tr in everyone if tr[0] == core and tr[7] == name)
@@ -131,6 +170,19 @@ def rank_program(g, core, T, topo):
             trs.append(RemoteDMATransfer(dst_ids=[DstId(rid=rid, pnc=pid)], dma_engine_mask=sum(1 << e for e in eng),
                                          remote_sem=sem[sn], src=T[sb][:, s0:s1], dst=T[db][:, d0:d1]))
         g.remote_dma_fused(trs, local_sem=sem.sent)
+
+    n_sent = sum(len(tr[8]) for trs in mine.values() for tr in trs)
+
+    if T.rank_of(core) is None:
+        g.wait_ge(sem.arl, expect("arl"))
+        emit("fw")
+        g.wait_ge(sem.sent, n_sent)
+        return
+
+    h = topo.host(core)
+    me, m = L[h], mem[h]
+    peers = [x for x in m if x != core]
+    role = "hs" if core == me["hs"] else ("hc" if core == me["hc"] else "sp")
 
     def bcol(host):
         return QP * T.rank_of(mem[host][0])
@@ -145,8 +197,8 @@ def rank_program(g, core, T, topo):
     g.wait_ge(sem.sz, 1)
     g.affine_select(T.ident[:], T.ones[:], [[-1, KP]], AluOpType.is_equal, 0.0, 0, 1).then_inc(sem.sid, 1)
 
-    g.sync.dma_start(T.kv[:, 0:KP], T.k[:]).then_inc(sem.ld1, 16)
-    g.scalar.dma_start(T.kv[:, KP:KV], T.v[:]).then_inc(sem.ld1, 16)
+    g.sync.dma_start(T.kv[:, KP:KV], T.v[:]).then_inc(sem.ldv, 16)
+    g.scalar.dma_start(T.kv[:, 0:KP], T.k[:]).then_inc(sem.ldk, 16)
     g.sync.dma_start(T.aux[:, HB:WIN], T.q[:]).then_inc(sem.ld2, 16)
     g.scalar.dma_start(T.aux[:, 0:HB], bsrc(me["far"])).then_inc(sem.ld2, 16)
     g.sync.dma_start(T.aux[:, WIN:WIN + HB], bsrc(me["sw"] if role == "hc" else me["cb"])).then_inc(sem.ld3, 16)
@@ -170,11 +222,14 @@ def rank_program(g, core, T, topo):
             g.sync.dma_start(T.rest[:, HB:2 * HB], bsrc(stay[1])).then_inc(sem.ld4, 16)
             n4 += 32
 
-    g.wait_ge(sem.ld1, 32)
-    emit("kvc")
-    emit("kvs")
+    g.wait_ge(sem.ldv, 16)
+    if role != "sp":
+        emit("vr")
+    g.wait_ge(sem.ldk, 16)
+    emit("kc")
     g.wait_ge(sem.ld2, 32)
     emit("fq")
+    emit("kvs")
     g.wait_ge(sem.ld3, n3)
     emit("win")
     emit("kvp")
@@ -192,15 +247,18 @@ def rank_program(g, core, T, topo):
     kv_j = [(cols("kvl", KV * j, KP), cols("kvl", KV * j + KP, KP)) for j in range(3)]
     q_me = cols("aux", HB, QP)
     b_own = cols("rest", where[h], HB)
+    bank_of, user = {}, {}
 
     def bias(u, bank, b):
+        if bank in user:
+            te.wait_ge(sem["r%d" % user[bank]], 1)
+        user[bank], bank_of[u] = u, bank
         te.matmul(T[bank][:, 0:HB], T.ident[:], b, True, False).then_inc(sem["t%d" % u], 1)
 
-    def scores(u, bank, q, kv):
+    def scores(u, q, kv):
+        bank = bank_of[u]
         for j in range(3):
             te.matmul(T[bank][:, QP * j:QP * j + QP], kv[j][0], q, False, j == 2).then_inc(sem["t%d" % u], 1)
-
-    def clamp(u, bank):
         ve.wait_ge(sem["t%d" % u], 4)
         ve.tensor_tensor(cols("s", HB * u, HB), T[bank][:, 0:HB], T.zero[:], AluOpType.max).then_inc(sem["r%d" % u], 1)
 
@@ -217,52 +275,55 @@ def rank_program(g, core, T, topo):
     te.wait_ge(sem.ld4, n4)
     if role != "sp":
         gs = _guests(core, cores, L, topo)
+        ng = len(gs)
         b_me = cols("rest", where[me["sw"] if role == "hs" else me["cb"]], HB)
-        bias(4, "p4", b_me)
-        te.wait_ge(sem.afq, expect("afq"))
-        for n in range(len(gs)):
-            bias(n, "p%d" % n, cols("fl", WIN * n, HB))
-        te.wait_ge(sem.akv, expect("akv"))
-        for n in range(len(gs)):
-            scores(n, "p%d" % n, cols("fl", WIN * n + HB, QP), kv_j)
-            clamp(n, "p%d" % n)
-        if len(gs) == 1:
-            scores(4, "p4", q_me, kv_j)
-        for n in range(len(gs)):
-            values(n, T.pof[:, QP * n:QP * n + QP], kv_j, sem.sof, True, True)
-        ve.wait_ge(sem.sof, 3 * len(gs))
-        ve.tensor_copy(T.ob[:, 0:QP * len(gs)], T.pof[:, 0:QP * len(gs)]).then_inc(sem.scf, 1)
-        g.wait_ge(sem.scf, 1)
-        emit("of")
+        s_k, s_v = ("akv", "akv") if role == "hs" else ("ak", "av")
+        if ng:
+            te.wait_ge(sem.afq, expect("afq"))
+            for n in range(ng):
+                bias(n, "p%d" % n, cols("fl", WIN * n, HB))
+        else:
+            bias(U_ME, "p0", b_me)
         te.wait_ge(sem.apw, expect("apw"))
         for n in range(2):
-            bias(2 + n, "p%d" % (2 + n), cols("pw", WIN * n + QP, HB))
-            scores(2 + n, "p%d" % (2 + n), cols("pw", WIN * n, QP), kv_j)
-            clamp(2 + n, "p%d" % (2 + n))
+            bias(GM + n, "p%d" % (GM + n), cols("pw", WIN * n + QP, HB))
+        te.wait_ge(sem[s_k], expect(s_k))
+        for n in range(ng):
+            scores(n, cols("fl", WIN * n + HB, QP), kv_j)
         for n in range(2):
-            values(2 + n, T.pop[:, QP * n:QP * n + QP], kv_j, sem.sop, True, True)
+            scores(GM + n, cols("pw", WIN * n, QP), kv_j)
+        if ng:
+            bias(U_ME, "p0", b_me)
+        scores(U_ME, q_me, kv_j)
+        te.wait_ge(sem[s_v], expect(s_v))
+        if ng:
+            for n in range(ng):
+                values(n, T.pof[:, QP * n:QP * n + QP], kv_j, sem.sof, True, True)
+            ve.wait_ge(sem.sof, 3 * ng)
+            ve.tensor_copy(T.ob[:, 0:QP * ng], T.pof[:, 0:QP * ng]).then_inc(sem.scf, 1)
+            g.wait_ge(sem.scf, 1)
+            emit("of")
+        for n in range(2):
+            values(GM + n, T.pop[:, QP * n:QP * n + QP], kv_j, sem.sop, True, True)
         ve.wait_ge(sem.sop, 6)
-        ve.tensor_copy(T.ob[:, 2 * QP:4 * QP], T.pop[:, 0:2 * QP]).then_inc(sem.scp, 1)
+        ve.tensor_copy(T.ob[:, GM * QP:(GM + 2) * QP], T.pop[:, 0:2 * QP]).then_inc(sem.scp, 1)
         g.wait_ge(sem.scp, 1)
         emit("op")
-        if len(gs) != 1:
-            scores(4, "p4", q_me, kv_j)
-        clamp(4, "p4")
-        te.wait_ge(sem.ld1, 32)
+        values(U_ME, y_acc, kv_j, sem.sos, True, False)
+        te.wait_ge(sem.ldk, 16)
+        te.wait_ge(sem.ldv, 16)
         te.wait_ge(sem.apk, expect("apk"))
-        bias(5, "p0", b_own)
-        scores(5, "p0", q_me, kv_own)
-        clamp(5, "p0")
-        values(4, y_acc, kv_j, sem.sos, True, False)
-        values(5, y_acc, kv_own, sem.sos, False, False)
+        bias(U_OWN, "p1", b_own)
+        scores(U_OWN, q_me, kv_own)
+        values(U_OWN, y_acc, kv_own, sem.sos, False, False)
         n_y += 6
     else:
-        bias(5, "p0", b_own)
-        te.wait_ge(sem.ld1, 32)
+        bias(U_OWN, "p0", b_own)
+        te.wait_ge(sem.ldk, 16)
+        te.wait_ge(sem.ldv, 16)
         te.wait_ge(sem.apk, expect("apk"))
-        scores(5, "p0", q_me, kv_own)
-        clamp(5, "p0")
-        values(5, y_acc, kv_own, sem.sos, True, False)
+        scores(U_OWN, q_me, kv_own)
+        values(U_OWN, y_acc, kv_own, sem.sos, True, False)
         n_y += 3
 
     late = 0 if len(_guests(me["hs"], cores, L, topo)) >= len(_guests(me["hc"], cores, L, topo)) else 1
@@ -281,4 +342,4 @@ def rank_program(g, core, T, topo):
     g.sync.wait_ge(sem.sy, 1)
     g.sync.dma_start(T.y[:], T.yb[:]).then_inc(sem.sst, 16)
     g.sync.wait_ge(sem.sst, 16)
-    g.wait_ge(sem.sent, sum(len(tr[8]) for trs in mine.values() for tr in trs))
+    g.wait_ge(sem.sent, n_sent)

@@ -26,18 +26,14 @@ SCRATCH = {
     "ones": ("sbuf", [128, KP], "bfloat16"),
     "ident": ("sbuf", [128, KP], "bfloat16"),
     "yb": ("sbuf", [128, QP], "bfloat16"),
-    "p0": ("psum", [128, 512], "float32"),
-    "p1": ("psum", [128, 512], "float32"),
-    "p2": ("psum", [128, 512], "float32"),
-    "p3": ("psum", [128, 512], "float32"),
-    "p4": ("psum", [128, 512], "float32"),
     "pos": ("psum", [128, 512], "float32"),
-    "pof": ("psum", [128, 512], "float32"),
-    "pop": ("psum", [128, 512], "float32"),
 }
-SEMAPHORES = (["ldk", "ldv", "ld2", "ld3", "ld4", "sz", "szero", "sid", "sent", "akv", "ak", "av", "arl", "afq", "apk",
-               "apw", "aoc0", "aoc1", "aof", "sof", "sop", "sos", "scf", "scp", "sy", "sst"]
-              + ["t%d" % u for u in range(NU)] + ["r%d" % u for u in range(NU)])
+for _u in range(NU):
+    SCRATCH["p%d" % _u] = ("psum", [128, 512], "float32")
+SEMAPHORES = (["ldk", "ldv", "ld2", "ld3", "ld4", "sz", "szero", "sel", "sid", "sent", "akv", "ak", "av", "arl", "afq",
+               "apk", "apw", "aoc0", "aoc1", "aof", "scp", "sos", "sy", "sst"]
+              + ["t%d" % u for u in range(NU)] + ["r%d" % u for u in range(NU)]
+              + ["o%d" % u for u in range(GM + 2)] + ["c%d" % u for u in range(GM)])
 
 
 def _bits(m):
@@ -95,7 +91,8 @@ def _target(c, L, topo):
 
 
 def _guests(x, cores, L, topo):
-    return [r for r in cores if _target(r, L, topo) == x]
+    gs = [r for r in cores if _target(r, L, topo) == x]
+    return sorted(gs, key=lambda r: len([p for p in cores if _target(p, L, topo) == r]))
 
 
 def _calls(c, cores, mem, L, topo):
@@ -106,35 +103,32 @@ def _calls(c, cores, mem, L, topo):
     chip = _bits(topo.mask(c, peers[0]) & topo.mask(c, peers[1]))
     off = [e for e in _bits(topo.mask(c, d_sw) & topo.mask(c, d_cb)) if e in chip]
     on = [e for e in chip if e not in off]
-    half = len(off) // 2
     i = m.index(c)
 
     def slot(x):
         return [p for p in m if p != x].index(c)
 
     out = {}
-    out["kvs"] = [(d_sw, "kv", 0, KV, "kvl", KV * i, KV * i + KV, "akv", off[0:half:2])]
     if c == me["sp"]:
-        out["kc"] = [(d_cb, "kv", 0, KV, "kvl", KV * i, KV * i + KV, "ak", off[1:half:2])]
+        out["kc"] = [(d_cb, "kv", 0, KV, "kvl", KV * i, KV * i + KV, "ak", off[0::2])]
     else:
-        out["kc"] = [(d_cb, "kv", 0, KP, "kvl", KV * i, KV * i + KP, "ak", off[1:half:2])]
+        out["kc"] = [(d_cb, "kv", 0, KP, "kvl", KV * i, KV * i + KP, "ak", off[0::2])]
         out["vr"] = [(me["relay"][c], "kv", KP, KV, "kv", KP, KV, "arl", on[0::2])]
     t = _target(c, L, topo)
     s = WIN * _guests(t, cores, L, topo).index(c)
-    out["fq"] = [(t, "aux", 0, WIN, "fl", s, s + WIN, "afq", off[half:])]
+    out["fq"] = [(t, "aux", 0, WIN, "fl", s, s + WIN, "afq", off[1::2])]
+    out["kvs"] = [(d_sw, "kv", 0, KV, "kvl", KV * i, KV * i + KV, "akv", off[1::2])]
     win = []
     if c != me["hc"]:
         win.append((me["hc"], "aux", HB, HB + WIN))
     if c != me["hs"]:
         win.append((me["hs"], "aux", HB, HB + WIN) if c == me["hc"] else (me["hs"], "aux2", 0, WIN))
-    out["win"] = [(x, sb, s0, s1, "pw", WIN * slot(x), WIN * slot(x) + WIN, "apw", off[n::len(win)])
+    out["win"] = [(x, sb, s0, s1, "pw", WIN * slot(x), WIN * slot(x) + WIN, "apw", on[(n + 1) % 2::2])
                   for n, (x, sb, s0, s1) in enumerate(win)]
     out["kvp"] = [(p, "kv", 0, KV, "pk", KV * slot(p), KV * slot(p) + KV, "apk", on[n::2]) for n, p in enumerate(peers)]
     if c != me["sp"]:
-        gs = _guests(c, cores, L, topo)
-        if gs:
-            out["of"] = [(r, "ob", QP * n, QP * n + QP, "ol", 2 * QP, 3 * QP, "aof", off[2 * n:2 * n + 2])
-                         for n, r in enumerate(gs)]
+        for n, r in enumerate(_guests(c, cores, L, topo)):
+            out["of%d" % n] = [(r, "ob", QP * n, QP * n + QP, "ol", 2 * QP, 3 * QP, "aof", off)]
         w = 0 if c == me["hs"] else 1
         out["op"] = [(p, "ob", QP * (GM + n), QP * (GM + n + 1), "ol", QP * w, QP * w + QP, "aoc%d" % w, on[n::2])
                      for n, p in enumerate(peers)]
@@ -147,7 +141,11 @@ def _plan(cores, mem, L, topo):
         d_cb = _handler(L, L[h]["cb"], h)
         for r, x in L[h]["relay"].items():
             o = KV * mem[h].index(r) + KP
-            plan[x] = {"fw": [(d_cb, "kv", KP, KV, "kvl", o, o + KP, "av", _bits(topo.mask(x, d_cb))[0:4])]}
+            eng = _bits(topo.mask(x, d_cb))
+            near = [p for p in mem[h] if topo.die(p) == topo.die(x)]
+            w = len(eng) // len(near)
+            plan[x] = {"id": [(p, "ident", 0, KP, "ident", 0, KP, "sid", eng[w * n:w * n + w]) for n, p in enumerate(near)],
+                       "fw": [(d_cb, "kv", KP, KV, "kvl", o, o + KP, "av", eng)]}
     return plan
 
 
@@ -172,8 +170,14 @@ def rank_program(g, core, T, topo):
         g.remote_dma_fused(trs, local_sem=sem.sent)
 
     n_sent = sum(len(tr[8]) for trs in mine.values() for tr in trs)
+    te, ve = g.tensor, g.vector
 
     if T.rank_of(core) is None:
+        ve.memset(T.ones[:], 1.0).then_inc(sem.sz, 1)
+        g.wait_ge(sem.sz, 1)
+        g.affine_select(T.ident[:], T.ones[:], [[-1, KP]], AluOpType.is_equal, 0.0, 0, 1).then_inc(sem.sel, 1)
+        g.wait_ge(sem.sel, 1)
+        emit("id")
         g.wait_ge(sem.arl, expect("arl"))
         emit("fw")
         g.wait_ge(sem.sent, n_sent)
@@ -190,12 +194,7 @@ def rank_program(g, core, T, topo):
     def bsrc(host, n=1):
         return T.b[:, bcol(host):bcol(host) + n * HB]
 
-    te, ve = g.tensor, g.vector
-
-    ve.memset(T.ones[:], 1.0).then_inc(sem.sz, 1)
     ve.memset(T.zero[:], 0.0).then_inc(sem.szero, 1)
-    g.wait_ge(sem.sz, 1)
-    g.affine_select(T.ident[:], T.ones[:], [[-1, KP]], AluOpType.is_equal, 0.0, 0, 1).then_inc(sem.sid, 1)
 
     g.sync.dma_start(T.kv[:, KP:KV], T.v[:]).then_inc(sem.ldv, 16)
     g.scalar.dma_start(T.kv[:, 0:KP], T.k[:]).then_inc(sem.ldk, 16)
@@ -229,9 +228,9 @@ def rank_program(g, core, T, topo):
     emit("kc")
     g.wait_ge(sem.ld2, 32)
     emit("fq")
-    emit("kvs")
     g.wait_ge(sem.ld3, n3)
     emit("win")
+    emit("kvs")
     emit("kvp")
 
     def cols(buf, c0, n):
@@ -247,78 +246,68 @@ def rank_program(g, core, T, topo):
     kv_j = [(cols("kvl", KV * j, KP), cols("kvl", KV * j + KP, KP)) for j in range(3)]
     q_me = cols("aux", HB, QP)
     b_own = cols("rest", where[h], HB)
-    bank_of, user = {}, {}
 
-    def bias(u, bank, b):
-        if bank in user:
-            te.wait_ge(sem["r%d" % user[bank]], 1)
-        user[bank], bank_of[u] = u, bank
-        te.matmul(T[bank][:, 0:HB], T.ident[:], b, True, False).then_inc(sem["t%d" % u], 1)
+    def bias(u, b):
+        te.matmul(cols("p%d" % u, 0, HB), T.ident[:], b, True, False).then_inc(sem["t%d" % u], 1)
 
     def scores(u, q, kv):
-        bank = bank_of[u]
         for j in range(3):
-            te.matmul(T[bank][:, QP * j:QP * j + QP], kv[j][0], q, False, j == 2).then_inc(sem["t%d" % u], 1)
+            te.matmul(cols("p%d" % u, QP * j, QP), kv[j][0], q, False, j == 2).then_inc(sem["t%d" % u], 1)
         ve.wait_ge(sem["t%d" % u], 4)
-        ve.tensor_tensor(cols("s", HB * u, HB), T[bank][:, 0:HB], T.zero[:], AluOpType.max).then_inc(sem["r%d" % u], 1)
+        ve.tensor_tensor(cols("s", HB * u, HB), cols("p%d" % u, 0, HB), T.zero[:],
+                         AluOpType.max).then_inc(sem["r%d" % u], 1)
 
     def values(u, out, kv, done, first, last):
         te.wait_ge(sem["r%d" % u], 1)
         for j in range(3):
             te.matmul(out, kv[j][1], cols("s", HB * u + QP * j, QP), first and j == 0, last and j == 2).then_inc(done, 1)
 
+    def block(u, done):
+        values(u, cols("p%d" % u, 0, QP), kv_j, sem["o%d" % u], True, True)
+        ve.wait_ge(sem["o%d" % u], 3)
+        ve.tensor_copy(cols("ob", QP * u, QP), cols("p%d" % u, 0, QP)).then_inc(done, 1)
+
     y_acc = T.pos[:, 0:QP]
     n_y = 0
-    te.wait_ge(sem.sid, 1)
+    te.wait_ge(sem.sid, expect("sid"))
     ve.wait_ge(sem.szero, 1)
     te.wait_ge(sem.ld2, 32)
     te.wait_ge(sem.ld4, n4)
+    bias(U_OWN, b_own)
     if role != "sp":
-        gs = _guests(core, cores, L, topo)
-        ng = len(gs)
-        b_me = cols("rest", where[me["sw"] if role == "hs" else me["cb"]], HB)
+        ng = len(_guests(core, cores, L, topo))
         s_k, s_v = ("akv", "akv") if role == "hs" else ("ak", "av")
+        bias(U_ME, cols("rest", where[me["sw"] if role == "hs" else me["cb"]], HB))
         if ng:
             te.wait_ge(sem.afq, expect("afq"))
             for n in range(ng):
-                bias(n, "p%d" % n, cols("fl", WIN * n, HB))
-        else:
-            bias(U_ME, "p0", b_me)
+                bias(n, cols("fl", WIN * n, HB))
         te.wait_ge(sem.apw, expect("apw"))
         for n in range(2):
-            bias(GM + n, "p%d" % (GM + n), cols("pw", WIN * n + QP, HB))
+            bias(GM + n, cols("pw", WIN * n + QP, HB))
         te.wait_ge(sem[s_k], expect(s_k))
         for n in range(ng):
             scores(n, cols("fl", WIN * n + HB, QP), kv_j)
         for n in range(2):
             scores(GM + n, cols("pw", WIN * n, QP), kv_j)
-        if ng:
-            bias(U_ME, "p0", b_me)
-        scores(U_ME, q_me, kv_j)
         te.wait_ge(sem[s_v], expect(s_v))
-        if ng:
-            for n in range(ng):
-                values(n, T.pof[:, QP * n:QP * n + QP], kv_j, sem.sof, True, True)
-            ve.wait_ge(sem.sof, 3 * ng)
-            ve.tensor_copy(T.ob[:, 0:QP * ng], T.pof[:, 0:QP * ng]).then_inc(sem.scf, 1)
-            g.wait_ge(sem.scf, 1)
-            emit("of")
+        for n in range(ng):
+            block(n, sem["c%d" % n])
+            g.wait_ge(sem["c%d" % n], 1)
+            emit("of%d" % n)
         for n in range(2):
-            values(GM + n, T.pop[:, QP * n:QP * n + QP], kv_j, sem.sop, True, True)
-        ve.wait_ge(sem.sop, 6)
-        ve.tensor_copy(T.ob[:, GM * QP:(GM + 2) * QP], T.pop[:, 0:2 * QP]).then_inc(sem.scp, 1)
-        g.wait_ge(sem.scp, 1)
+            block(GM + n, sem.scp)
+        g.wait_ge(sem.scp, 2)
         emit("op")
-        values(U_ME, y_acc, kv_j, sem.sos, True, False)
+        scores(U_ME, q_me, kv_j)
         te.wait_ge(sem.ldk, 16)
         te.wait_ge(sem.ldv, 16)
         te.wait_ge(sem.apk, expect("apk"))
-        bias(U_OWN, "p1", b_own)
         scores(U_OWN, q_me, kv_own)
+        values(U_ME, y_acc, kv_j, sem.sos, True, False)
         values(U_OWN, y_acc, kv_own, sem.sos, False, False)
         n_y += 6
     else:
-        bias(U_OWN, "p0", b_own)
         te.wait_ge(sem.ldk, 16)
         te.wait_ge(sem.ldv, 16)
         te.wait_ge(sem.apk, expect("apk"))

from concourse.bass import DstId, RemoteDMATransfer
from concourse.mybir import AluOpType

QP = 64
KP = 128
HB = 3 * QP
KV = 2 * KP
WIN = QP + HB
GM = 3
NU = GM + 4
U_ME, U_OWN = GM + 2, GM + 3

SCRATCH = {
    "kv": ("sbuf", [128, KV], "bfloat16"),
    "aux": ("sbuf", [128, HB + WIN], "bfloat16"),
    "aux2": ("sbuf", [128, WIN], "bfloat16"),
    "rest": ("sbuf", [128, 2 * HB], "bfloat16"),
    "kvl": ("sbuf", [128, 3 * KV], "bfloat16"),
    "pk": ("sbuf", [128, 2 * KV], "bfloat16"),
    "pw": ("sbuf", [128, 2 * WIN], "bfloat16"),
    "fl": ("sbuf", [128, GM * WIN], "bfloat16"),
    "ol": ("sbuf", [128, 3 * QP], "bfloat16"),
    "ob": ("sbuf", [128, (GM + 2) * QP], "bfloat16"),
    "s": ("sbuf", [128, NU * HB], "bfloat16"),
    "zero": ("sbuf", [128, HB], "float32"),
    "ones": ("sbuf", [128, KP], "bfloat16"),
    "ident": ("sbuf", [128, KP], "bfloat16"),
    "yb": ("sbuf", [128, QP], "bfloat16"),
    "pos": ("psum", [128, 512], "float32"),
}
for _u in range(NU):
    SCRATCH["p%d" % _u] = ("psum", [128, 512], "float32")
SEMAPHORES = (["ldk", "ldv", "ld2", "ld3", "ld4", "sz", "szero", "sel", "sid", "sent", "akv", "ak", "av", "arl", "afq",
               "apk", "apw", "aoc0", "aoc1", "aof", "scp", "sos", "sy", "sst"]
              + ["t%d" % u for u in range(NU)] + ["r%d" % u for u in range(NU)]
              + ["o%d" % u for u in range(GM + 2)] + ["c%d" % u for u in range(GM)])


def _bits(m):
    return [e for e in range(m.bit_length()) if (m >> e) & 1]


def _chip_cores(c, topo):
    def here(x):
        return x >= 0 and (topo.host(x), topo.chip(x)) == (topo.host(c), topo.chip(c))
    lo, hi = c, c
    while here(lo - 1):
        lo -= 1
    while here(hi + 1):
        hi += 1
    mate = [x for x in (lo - 1, hi + 1) if x >= 0 and topo.mates(c, x)][0]
    return list(range(lo, hi + 1)), mate


def _layout(T, topo):
    cores = list(T.cores)
    hosts = sorted(set(topo.host(c) for c in cores))
    mem = {h: [c for c in cores if topo.host(c) == h] for h in hosts}
    L = {}
    for h in hosts:
        m = mem[h]
        near = [x for x in hosts if x != h and topo.may_write(m[0], mem[x][0])]
        order = sorted(m, key=lambda c: (-len([x for x in m if topo.die(x) == topo.die(c)]), m.index(c)))
        chip, mate = _chip_cores(m[0], topo)

        def pair(x):
            return (topo.die(x), topo.may_write(x, mate))

        taken = [pair(x) for x in m]
        free = []
        for x in chip:
            if pair(x) not in taken:
                taken.append(pair(x))
                free.append(x)
        free.sort(key=lambda x: topo.die(x) != topo.die(order[0]))
        L[h] = {"sw": [x for x in near if topo.rack(x) == topo.rack(h)][0],
                "cb": [x for x in near if topo.rack(x) != topo.rack(h)][0],
                "far": [x for x in hosts if x != h and x not in near][0],
                "hs": order[0], "hc": order[1], "sp": order[2],
                "relay": {order[0]: free[0], order[1]: free[1]}}
    return cores, mem, L


def _handler(L, at, of):
    return L[at]["hs"] if L[at]["sw"] == of else L[at]["hc"]


def _target(c, L, topo):
    me = L[topo.host(c)]
    return _handler(L, me["sw"], me["far"])


def _guests(x, cores, L, topo):
    gs = [r for r in cores if _target(r, L, topo) == x]
    return sorted(gs, key=lambda r: len([p for p in cores if _target(p, L, topo) == r]))


def _calls(c, cores, mem, L, topo):
    h = topo.host(c)
    me, m = L[h], mem[h]
    peers = [x for x in m if x != c]
    d_sw, d_cb = _handler(L, me["sw"], h), _handler(L, me["cb"], h)
    chip = _bits(topo.mask(c, peers[0]) & topo.mask(c, peers[1]))
    off = [e for e in _bits(topo.mask(c, d_sw) & topo.mask(c, d_cb)) if e in chip]
    on = [e for e in chip if e not in off]
    i = m.index(c)

    def slot(x):
        return [p for p in m if p != x].index(c)

    out = {}
    if c == me["sp"]:
        out["kc"] = [(d_cb, "kv", 0, KV, "kvl", KV * i, KV * i + KV, "ak", off[0::2])]
    else:
        out["kc"] = [(d_cb, "kv", 0, KP, "kvl", KV * i, KV * i + KP, "ak", off[0::2])]
        out["vr"] = [(me["relay"][c], "kv", KP, KV, "kv", KP, KV, "arl", on[0::2])]
    t = _target(c, L, topo)
    s = WIN * _guests(t, cores, L, topo).index(c)
    out["fq"] = [(t, "aux", 0, WIN, "fl", s, s + WIN, "afq", off[1::2])]
    out["kvs"] = [(d_sw, "kv", 0, KV, "kvl", KV * i, KV * i + KV, "akv", off[1::2])]
    win = []
    if c != me["hc"]:
        win.append((me["hc"], "aux", HB, HB + WIN))
    if c != me["hs"]:
        win.append((me["hs"], "aux", HB, HB + WIN) if c == me["hc"] else (me["hs"], "aux2", 0, WIN))
    out["win"] = [(x, sb, s0, s1, "pw", WIN * slot(x), WIN * slot(x) + WIN, "apw", on[(n + 1) % 2::2])
                  for n, (x, sb, s0, s1) in enumerate(win)]
    out["kvp"] = [(p, "kv", 0, KV, "pk", KV * slot(p), KV * slot(p) + KV, "apk", on[n::2]) for n, p in enumerate(peers)]
    if c != me["sp"]:
        for n, r in enumerate(_guests(c, cores, L, topo)):
            out["of%d" % n] = [(r, "ob", QP * n, QP * n + QP, "ol", 2 * QP, 3 * QP, "aof", off)]
        w = 0 if c == me["hs"] else 1
        out["op"] = [(p, "ob", QP * (GM + n), QP * (GM + n + 1), "ol", QP * w, QP * w + QP, "aoc%d" % w, on[n::2])
                     for n, p in enumerate(peers)]
    return out


def _plan(cores, mem, L, topo):
    plan = {c: _calls(c, cores, mem, L, topo) for c in cores}
    for h in L:
        d_cb = _handler(L, L[h]["cb"], h)
        for r, x in L[h]["relay"].items():
            o = KV * mem[h].index(r) + KP
            eng = _bits(topo.mask(x, d_cb))
            near = [p for p in mem[h] if topo.die(p) == topo.die(x)]
            w = len(eng) // len(near)
            plan[x] = {"id": [(p, "ident", 0, KP, "ident", 0, KP, "sid", eng[w * n:w * n + w]) for n, p in enumerate(near)],
                       "fw": [(d_cb, "kv", KP, KV, "kvl", o, o + KP, "av", eng)]}
    return plan


def rank_program(g, core, T, topo):
    cores, mem, L = _layout(T, topo)
    plan = _plan(cores, mem, L, topo)
    if core not in plan:
        return
    sem = T.sem
    mine = plan[core]
    everyone = [tr for calls in plan.values() for trs in calls.values() for tr in trs]

    def expect(name):
        return sum(len(tr[8]) for tr in everyone if tr[0] == core and tr[7] == name)

    def emit(name):
        trs = []
        for (d, sb, s0, s1, db, d0, d1, sn, eng) in mine[name]:
            rid, pid = topo.addr(d, core)
            trs.append(RemoteDMATransfer(dst_ids=[DstId(rid=rid, pnc=pid)], dma_engine_mask=sum(1 << e for e in eng),
                                         remote_sem=sem[sn], src=T[sb][:, s0:s1], dst=T[db][:, d0:d1]))
        g.remote_dma_fused(trs, local_sem=sem.sent)

    n_sent = sum(len(tr[8]) for trs in mine.values() for tr in trs)
    te, ve = g.tensor, g.vector

    if T.rank_of(core) is None:
        ve.memset(T.ones[:], 1.0).then_inc(sem.sz, 1)
        g.wait_ge(sem.sz, 1)
        g.affine_select(T.ident[:], T.ones[:], [[-1, KP]], AluOpType.is_equal, 0.0, 0, 1).then_inc(sem.sel, 1)
        g.wait_ge(sem.sel, 1)
        emit("id")
        g.wait_ge(sem.arl, expect("arl"))
        emit("fw")
        g.wait_ge(sem.sent, n_sent)
        return

    h = topo.host(core)
    me, m = L[h], mem[h]
    peers = [x for x in m if x != core]
    role = "hs" if core == me["hs"] else ("hc" if core == me["hc"] else "sp")

    def bcol(host):
        return QP * T.rank_of(mem[host][0])

    def bsrc(host, n=1):
        return T.b[:, bcol(host):bcol(host) + n * HB]

    ve.memset(T.zero[:], 0.0).then_inc(sem.szero, 1)

    g.sync.dma_start(T.kv[:, KP:KV], T.v[:]).then_inc(sem.ldv, 16)
    g.scalar.dma_start(T.kv[:, 0:KP], T.k[:]).then_inc(sem.ldk, 16)
    g.sync.dma_start(T.aux[:, HB:WIN], T.q[:]).then_inc(sem.ld2, 16)
    g.scalar.dma_start(T.aux[:, 0:HB], bsrc(me["far"])).then_inc(sem.ld2, 16)
    g.sync.dma_start(T.aux[:, WIN:WIN + HB], bsrc(me["sw"] if role == "hc" else me["cb"])).then_inc(sem.ld3, 16)
    n3, n4 = 16, 0
    where = {}
    if role == "sp":
        g.scalar.dma_start(T.aux2[:, 0:QP], T.q[:]).then_inc(sem.ld3, 16)
        g.sync.dma_start(T.aux2[:, QP:WIN], bsrc(me["sw"])).then_inc(sem.ld3, 16)
        n3 += 32
        g.scalar.dma_start(T.rest[:, 0:HB], bsrc(h)).then_inc(sem.ld4, 16)
        n4 += 16
        where[h] = 0
    else:
        stay = sorted([h, me["sw"] if role == "hs" else me["cb"]], key=bcol)
        where[stay[0]], where[stay[1]] = 0, HB
        if bcol(stay[1]) - bcol(stay[0]) == HB:
            g.scalar.dma_start(T.rest[:], bsrc(stay[0], 2)).then_inc(sem.ld4, 16)
            n4 += 16
        else:
            g.scalar.dma_start(T.rest[:, 0:HB], bsrc(stay[0])).then_inc(sem.ld4, 16)
            g.sync.dma_start(T.rest[:, HB:2 * HB], bsrc(stay[1])).then_inc(sem.ld4, 16)
            n4 += 32

    g.wait_ge(sem.ldv, 16)
    if role != "sp":
        emit("vr")
    g.wait_ge(sem.ldk, 16)
    emit("kc")
    g.wait_ge(sem.ld2, 32)
    emit("fq")
    g.wait_ge(sem.ld3, n3)
    emit("win")
    emit("kvs")
    emit("kvp")

    def cols(buf, c0, n):
        return T[buf][:, c0:c0 + n]

    kv_own = []
    for x in m:
        if x == core:
            kv_own.append((cols("kv", 0, KP), cols("kv", KP, KP)))
        else:
            o = KV * peers.index(x)
            kv_own.append((cols("pk", o, KP), cols("pk", o + KP, KP)))
    kv_j = [(cols("kvl", KV * j, KP), cols("kvl", KV * j + KP, KP)) for j in range(3)]
    q_me = cols("aux", HB, QP)
    b_own = cols("rest", where[h], HB)

    def bias(u, b):
        te.matmul(cols("p%d" % u, 0, HB), T.ident[:], b, True, False).then_inc(sem["t%d" % u], 1)

    def scores(u, q, kv):
        for j in range(3):
            te.matmul(cols("p%d" % u, QP * j, QP), kv[j][0], q, False, j == 2).then_inc(sem["t%d" % u], 1)
        ve.wait_ge(sem["t%d" % u], 4)
        ve.tensor_tensor(cols("s", HB * u, HB), cols("p%d" % u, 0, HB), T.zero[:],
                         AluOpType.max).then_inc(sem["r%d" % u], 1)

    def values(u, out, kv, done, first, last):
        te.wait_ge(sem["r%d" % u], 1)
        for j in range(3):
            te.matmul(out, kv[j][1], cols("s", HB * u + QP * j, QP), first and j == 0, last and j == 2).then_inc(done, 1)

    def block(u, done):
        values(u, cols("p%d" % u, 0, QP), kv_j, sem["o%d" % u], True, True)
        ve.wait_ge(sem["o%d" % u], 3)
        ve.tensor_copy(cols("ob", QP * u, QP), cols("p%d" % u, 0, QP)).then_inc(done, 1)

    y_acc = T.pos[:, 0:QP]
    n_y = 0
    te.wait_ge(sem.sid, expect("sid"))
    ve.wait_ge(sem.szero, 1)
    te.wait_ge(sem.ld2, 32)
    te.wait_ge(sem.ld4, n4)
    bias(U_OWN, b_own)
    if role != "sp":
        ng = len(_guests(core, cores, L, topo))
        s_k, s_v = ("akv", "akv") if role == "hs" else ("ak", "av")
        bias(U_ME, cols("rest", where[me["sw"] if role == "hs" else me["cb"]], HB))
        if ng:
            te.wait_ge(sem.afq, expect("afq"))
            for n in range(ng):
                bias(n, cols("fl", WIN * n, HB))
        te.wait_ge(sem.apw, expect("apw"))
        for n in range(2):
            bias(GM + n, cols("pw", WIN * n + QP, HB))
        te.wait_ge(sem[s_k], expect(s_k))
        for n in range(ng):
            scores(n, cols("fl", WIN * n + HB, QP), kv_j)
        for n in range(2):
            scores(GM + n, cols("pw", WIN * n, QP), kv_j)
        te.wait_ge(sem[s_v], expect(s_v))
        for n in range(ng):
            block(n, sem["c%d" % n])
            g.wait_ge(sem["c%d" % n], 1)
            emit("of%d" % n)
        for n in range(2):
            block(GM + n, sem.scp)
        g.wait_ge(sem.scp, 2)
        emit("op")
        scores(U_ME, q_me, kv_j)
        te.wait_ge(sem.ldk, 16)
        te.wait_ge(sem.ldv, 16)
        te.wait_ge(sem.apk, expect("apk"))
        scores(U_OWN, q_me, kv_own)
        values(U_ME, y_acc, kv_j, sem.sos, True, False)
        values(U_OWN, y_acc, kv_own, sem.sos, False, False)
        n_y += 6
    else:
        te.wait_ge(sem.ldk, 16)
        te.wait_ge(sem.ldv, 16)
        te.wait_ge(sem.apk, expect("apk"))
        scores(U_OWN, q_me, kv_own)
        values(U_OWN, y_acc, kv_own, sem.sos, True, False)
        n_y += 3

    late = 0 if len(_guests(me["hs"], cores, L, topo)) >= len(_guests(me["hc"], cores, L, topo)) else 1
    idx = {"hs": 0, "hc": 1, "sp": 2}[role]
    last = late if idx != late else 1 - late
    if role == "sp":
        te.wait_ge(sem["aoc%d" % (1 - late)], expect("aoc%d" % (1 - late)))
        te.matmul(y_acc, T.ident[:], cols("ol", QP * (1 - late), QP), False, False).then_inc(sem.sos, 1)
        n_y += 1
    te.wait_ge(sem.aof, expect("aof"))
    te.matmul(y_acc, T.ident[:], cols("ol", 2 * QP, QP), False, True).then_inc(sem.sos, 1)
    n_y += 1
    ve.wait_ge(sem.sos, n_y)
    ve.wait_ge(sem["aoc%d" % last], expect("aoc%d" % last))
    ve.tensor_tensor(T.yb[:], y_acc, cols("ol", QP * last, QP), AluOpType.add).then_inc(sem.sy, 1)
    g.sync.wait_ge(sem.sy, 1)
    g.sync.dma_start(T.y[:], T.yb[:]).then_inc(sem.sst, 16)
    g.sync.wait_ge(sem.sst, 16)
    g.wait_ge(sem.sent, n_sent)
